import numpy as np
import ml_dtypes


def mxq(x, axis, fmt="e4m3"):
    dtype, down = {"e4m3": (ml_dtypes.float8_e4m3fn, 7), "e5m2": (ml_dtypes.float8_e5m2, 14)}[fmt]
    v = np.moveaxis(np.asarray(x, np.float32).astype(ml_dtypes.bfloat16).astype(np.float64), axis, -1)
    blocks = v.reshape(v.shape[:-1] + (-1, 32))
    amax = np.abs(blocks).max(-1, keepdims=True)
    byte = np.maximum(np.where(amax > 0, np.frexp(amax)[1] - 1 + 127, 0) - down, 1)
    scale = np.exp2(byte - 127.0)
    codes = (blocks / scale).astype(np.float32).astype(dtype).astype(np.float64)
    return np.moveaxis((codes * scale).reshape(v.shape), -1, axis)


WIDE = False


def mx_kscale(k):
    if not WIDE:
        return np.ones(k)
    levels = np.array([10, -10, 5, -5, 0])
    if k % 512:
        return np.exp2(np.random.permutation(np.resize(levels, k // 32))).repeat(32)
    a = np.empty((k // 512, 16))
    for p in range(k // 512):
        a[p, :8] = np.random.permutation(np.resize(levels, 8))
        for g in range(8):
            far = levels[np.abs(levels - a[p, g]) >= 10]
            a[p, g + 8] = far[np.random.randint(len(far))]
    return np.exp2(a.ravel()).repeat(32)


def f64(x):
    return np.asarray(x).astype(np.float64)


def striped(idx):
    return np.tile(idx.reshape(-1, 16).T, (8, 1)).astype(np.uint16)


def unstriped(offs):
    return offs[:16].T.reshape(-1).astype(np.int64)


def pack_weight(w):
    k, n = w.shape
    w = f64(np.asarray(w, np.float32).astype(ml_dtypes.bfloat16)).reshape(k // 32, 32, n)
    amax = np.abs(w).max(1)
    byte = np.clip(np.where(amax > 0, np.frexp(amax)[1] - 1 + 127 - 7, 1), 1, 254)
    scaled = (w * np.exp2(127.0 - byte)[:, None, :]).reshape(k, n).astype(np.float32)
    words = np.ascontiguousarray(scaled.reshape(k // 512, 128, 4, n).transpose(0, 1, 3, 2)).astype(ml_dtypes.float8_e4m3fn).view(np.uint8)
    return words, np.ascontiguousarray(byte.astype(np.uint8).reshape(k // 512, 16, n))


def unpack_weight(words, scales):
    g, p, n, _ = words.shape
    vals = np.ascontiguousarray(words).view(ml_dtypes.float8_e4m3fn).astype(np.float64) * np.repeat(np.exp2(scales.astype(np.float64) - 127.0), 8, axis=1)[..., None]
    return vals.transpose(0, 1, 3, 2).reshape(g * 512, n)


def sigmoid(v):
    return 1.0 / (1.0 + np.exp(-np.maximum(v, -700.0)))


K, T, S, N, H, W = 512, 2048, 256, 512, 512, 1024


def setup_inputs():
    n = np.random.standard_normal
    s = mx_kscale(K)[:, None]
    u = mx_kscale(H)
    packed_xT = pack_weight(n((K, T)) * s)
    return {
        "x_words": packed_xT[0],
        "x_scales": packed_xT[1],
        "w1": (n((K, H)) / np.sqrt(K) / s).astype(np.float32),
        "w2": (n((K, H)) / np.sqrt(K) / s).astype(np.float32),
        "gn": (np.random.uniform(0.5, 1.5, (H, 1)) * u[:, None]).astype(np.float32),
        "w3": (n((H, N)) / np.sqrt(H) / u[:, None]).astype(np.float32),
        "offs": striped(np.random.permutation(T)[:S]),
        "two": striped(np.random.permutation(T)[:S]),
        "n1": striped(np.random.permutation(S)),
        "n2": striped(np.random.permutation(S)),
        "n3": striped(np.random.permutation(S)),
        "n4": striped(np.random.randint(0, S, W)),
    }


def reference(x_words, x_scales, w1, w2, gn, w3, offs, two, n1, n2, n3, n4):
    x_two = unpack_weight(x_words, x_scales)[:, unstriped(two)]
    d = mxq(f64(w2), 0, "e4m3").T @ x_two
    xq = unpack_weight(x_words, x_scales)[:, unstriped(offs)]
    y = mxq(f64(w1), 0, "e4m3").T @ xq
    z = f64(gn) * (d * (y[:, unstriped(n1)] - y) + 0.5 * (d[:, unstriped(n3)] * (y[:, unstriped(n2)] - y)))
    h = mxq(f64(w3), 0, "e4m3").T @ mxq(z, 0, "e4m3")
    mb = h[:, unstriped(n4)]
    ms = mb.reshape(N, S, 4).sum(axis=2)
    return h * sigmoid(ms)

@@ -1,0 +1,230 @@
+from contextlib import ExitStack
+
+import concourse.mybir as mybir
+
+K, T, S, N, H, W = 512, 2048, 256, 512, 512, 1024
+FLOPS = 2 * K * H * S * 2 + 2 * H * N * S
+
+F32 = mybir.dt.float32
+BF16 = mybir.dt.bfloat16
+I32 = mybir.dt.int32
+U32 = mybir.dt.uint32
+U16 = mybir.dt.uint16
+U8 = mybir.dt.uint8
+FP8X4 = mybir.dt.float8_e4m3fn_x4
+ALU = mybir.AluOpType
+ACT = mybir.ActivationFunctionType
+
+P = 128
+PACK = 4
+SPARE = 16
+MEMBERS = 4
+W1_VECTOR = 80
+ON_VECTOR = ((0, 2), (0, 3), (1, 3), (2, 3), (3, 3))
+
+
+def tile_picked_twlflowbgsumg_none_p_kernel(
+    tc, x_words, x_scales, w1, w2, gn, w3, offs, two, n1, n2, n3, n4, out
+):
+    nc = tc.nc
+    with ExitStack() as ctx:
+        keep = ctx.enter_context(tc.tile_pool(name="keep", bufs=1))
+        psum = ctx.enter_context(tc.psum_pool(name="psum", bufs=1))
+
+        def load_list(src, name):
+            lst = keep.tile([P, src.shape[1]], U16, name=name)
+            nc.sync.dma_start(lst[:], src)
+            return lst
+
+        def load_weight(src, name):
+            raw = keep.tile([P, PACK, src.shape[1]], F32, name=name, tag=name)
+            nc.sync.dma_start(out=raw[:], in_=src.rearrange("(p j) c -> p j c", j=PACK))
+            return raw
+
+        def mx_tiles(width, name, tag=""):
+            rounded = keep.tile([P, PACK * width], BF16, name=name + "_bf16", tag=tag or name + "_bf16", align_bytes=64)
+            codes = keep.tile([P, width], U32, name=name + "_codes", tag=name + "_codes", align_bytes=64)
+            scales = keep.tile([P, width], U8, name=name + "_scales", align_bytes=64)
+            return rounded, codes, scales
+
+        def quantize(tiles, first, count):
+            rounded, codes, scales = tiles
+            nc.vector.quantize_mx(
+                out=codes[:, first : first + count].bitcast(FP8X4),
+                scales=scales[:, first : first + count],
+                in_=rounded[:, PACK * first : PACK * (first + count)],
+            )
+
+        def deal(copy, raw, rounded, m0, m1):
+            copy(
+                out=rounded[:].rearrange("p (t m j) -> p m j t", t=PACK, j=PACK)[:, m0:m1],
+                in_=raw[:].rearrange("p j (m t) -> p m j t", t=PACK)[:, m0:m1],
+            )
+
+        def product(bank, w_tiles, t, codes, scales):
+            nc.tensor.matmul_mx(
+                out=bank[:],
+                lhsT=w_tiles[1][:, t * P : (t + 1) * P].bitcast(FP8X4),
+                lhsT_scale=w_tiles[2][:, t * P : (t + 1) * P],
+                rhs=codes[:].bitcast(FP8X4),
+                rhs_scale=scales[:],
+                start=True,
+                stop=True,
+            )
+
+        def window(name):
+            win = keep.tile([P, S + SPARE], F32, name=name)
+            nc.gpsimd.memset(win[:, S:], 0.0)
+            return win
+
+        xs = keep.tile([P, T], U8, name="xs")
+        nc.vector.memset(xs[:].bitcast(I32), 0)
+        for q in range(4):
+            nc.scalar.dma_start(
+                out=xs[32 * q : 32 * q + 4, :].bitcast(I32), in_=x_scales[0, 4 * q : 4 * q + 4, :].bitcast(I32)
+            )
+        offs_l = load_list(offs, "offs_l")
+        w1_raw = load_weight(w1, "w1_raw")
+        two_l = load_list(two, "two_l")
+        xw = keep.tile([P, T], I32, name="xw")
+        nc.sync.dma_start(out=xw[:], in_=x_words[0].rearrange("p n t -> p (n t)").bitcast(I32))
+        n1_l = load_list(n1, "n1_l")
+        n2_l = load_list(n2, "n2_l")
+        w2_raw = load_weight(w2, "w2_raw")
+        n3_l = load_list(n3, "n3_l")
+        gain = keep.tile([P, PACK], F32, name="gain")
+        nc.sync.dma_start(out=gain[:], in_=gn.rearrange("(p t) o -> p (t o)", t=PACK))
+        w3_raw = load_weight(w3, "w3_raw")
+        n4_l = load_list(n4, "n4_l")
+
+        y_win = [window(f"y_win{t}") for t in range(PACK)]
+        d_win = [window(f"d_win{t}") for t in range(PACK)]
+        h_win = [window(f"h_win{t}") for t in range(PACK)]
+        half_gain = keep.tile([P, PACK], F32, name="half_gain")
+        nc.gpsimd.tensor_scalar(half_gain[:], gain[:], 0.5, 0.0, ALU.mult, ALU.add)
+
+        xy_codes = keep.tile([P, S], U32, name="xy_codes", align_bytes=64)
+        xy_scales = keep.tile([P, S], U8, name="xy_scales", align_bytes=64)
+        xd_codes = keep.tile([P, S], U32, name="xd_codes", align_bytes=64)
+        xd_scales = keep.tile([P, S], U8, name="xd_scales", align_bytes=64)
+        w1_mx = mx_tiles(H, "w1")
+        w2_mx = mx_tiles(H, "w2")
+        z_mx = mx_tiles(S, "z")
+
+        nc.vector.tensor_copy(xy_scales[:], xs[:].indirect(offs_l[:]))
+        deal(nc.vector.tensor_copy, w1_raw, w1_mx[0], 0, W1_VECTOR)
+        deal(nc.scalar.copy, w1_raw, w1_mx[0], W1_VECTOR, P)
+        quantize(w1_mx, 0, H)
+        nc.vector.tensor_copy(xd_scales[:], xs[:].indirect(two_l[:]))
+        nc.vector.tensor_copy(xy_codes[:], xw[:].bitcast(U32).indirect(offs_l[:]))
+        nc.vector.tensor_copy(xd_codes[:], xw[:].bitcast(U32).indirect(two_l[:]))
+        y_bank = [psum.tile([P, S], F32, name=f"y_bank{t}", tag=f"bank{t}") for t in range(PACK)]
+        for t in range(PACK):
+            product(y_bank[t], w1_mx, t, xy_codes, xy_scales)
+        nc.scalar.copy(y_win[0][:, :S], y_bank[0][:])
+        for t in (1, 2):
+            nc.vector.tensor_copy(y_win[t][:, :S], y_bank[t][:])
+
+        early = keep.tile([P, 2, 2, S], F32, name="early")
+        pair = [early[:, 0], early[:, 1]]
+        near = keep.tile([P, PACK, S], F32, name="near")
+        far = keep.tile([P, PACK, S], F32, name="far")
+
+        def fetch_y(t):
+            nc.scalar.activation(pair[t][:, 0], y_win[t][:].indirect(n1_l[:]), ACT.Copy)
+            nc.scalar.activation(pair[t][:, 1], y_win[t][:].indirect(n2_l[:]), ACT.Copy)
+
+        fetch_y(0)
+        deal(nc.vector.tensor_copy, w2_raw, w2_mx[0], 0, P)
+        fetch_y(1)
+        nc.scalar.copy(y_win[3][:, :S], y_bank[3][:])
+        d_bank = [psum.tile([P, S], F32, name=f"d_bank{t}", tag=f"bank{PACK + t}") for t in range(PACK)]
+        for t in range(PACK):
+            quantize(w2_mx, t * P, P)
+            product(d_bank[t], w2_mx, t, xd_codes, xd_scales)
+
+        late = keep.tile([P, 2, 2, S], F32, name="late", tag="w2_bf16", align_bytes=64)
+        pair.extend([late[:, 0], late[:, 1]])
+        diffs = keep.tile([P, 2 * PACK, S], F32, name="diffs", tag="w2_raw")
+        diff = [diffs[:, i] for i in range(2 * PACK)]
+        w3_mx = mx_tiles(N, "w3", tag="w2_codes")
+        w3_dst = w3_mx[0][:].rearrange("p (c i j) -> p c j i", i=4, j=PACK)
+        w3_src = w3_raw[:].rearrange("p j (c i) -> p c j i", i=4)
+        for t in range(PACK):
+            nc.scalar.activation(d_win[t][:, :S], d_bank[t][:], ACT.Copy, scale=half_gain[:, t : t + 1])
+        fetch_y(2)
+        fetch_y(3)
+        for t in range(PACK):
+            for u in range(2):
+                nc.vector.tensor_tensor(diff[2 * t + u], pair[t][:, u], y_win[t][:, :S], ALU.subtract)
+            nc.vector.scalar_tensor_tensor(near[:, t, :], diff[2 * t], 2.0, d_win[t][:, :S], ALU.mult, ALU.mult)
+            nc.vector.tensor_tensor(far[:, t, :], d_win[t][:].indirect(n3_l[:]), diff[2 * t + 1], ALU.mult)
+        for half in range(2):
+            nc.scalar.copy(out=w3_dst[:, half * 64 : (half + 1) * 64], in_=w3_src[:, half * 64 : (half + 1) * 64])
+        z_dst = z_mx[0][:].rearrange("p (c i t) -> p c t i", i=4, t=PACK)
+        near_src = near[:].rearrange("p t (c i) -> p c t i", i=4)
+        far_src = far[:].rearrange("p t (c i) -> p c t i", i=4)
+        for half in range(2):
+            cs = slice(half * 32, (half + 1) * 32)
+            nc.vector.tensor_tensor(z_dst[:, cs], near_src[:, cs], far_src[:, cs], ALU.add)
+            quantize(w3_mx, half * 256, 256)
+        for half in range(2):
+            quantize(z_mx, half * P, P)
+
+        h_bank = [psum.tile([P, S], F32, name=f"h_bank{u}", tag=f"bank{u}") for u in range(PACK)]
+        for u in range(PACK):
+            product(h_bank[u], w3_mx, u, z_mx[1], z_mx[2])
+        members = [keep.tile([P, W], F32, name=f"members{u}") for u in range(PACK)]
+        pairs = [keep.tile([P, W // 2], F32, name=f"pairs{u}") for u in range(PACK)]
+        sums = [keep.tile([P, S], F32, name=f"sums{u}") for u in range(PACK)]
+        gate = [keep.tile([P, S], F32, name=f"gate{u}") for u in range(PACK)]
+        result = [keep.tile([P, S], F32, name=f"result{u}") for u in range(PACK)]
+
+        def halve_h(u):
+            if u == 1:
+                nc.vector.tensor_scalar(h_win[u][:, :S], h_bank[u][:], 0.5, 0.0, ALU.mult, ALU.add)
+            else:
+                nc.scalar.activation(h_win[u][:, :S], h_bank[u][:], ACT.Copy, scale=0.5)
+
+        def fetch_h(u, quarters):
+            for q in quarters:
+                looked_up = h_win[u][:].indirect(n4_l[:, q * 16 : (q + 1) * 16])
+                dst = members[u][:, q * S : (q + 1) * S]
+                if (u, q) in ON_VECTOR:
+                    nc.vector.tensor_copy(dst, looked_up)
+                else:
+                    nc.scalar.activation(dst, looked_up, ACT.Copy)
+
+        def add_pairs(u, j0, j1):
+            m4 = members[u][:].rearrange("p (j t) -> p j t", t=MEMBERS)[:, j0:j1]
+            nc.vector.tensor_tensor(
+                pairs[u][:].rearrange("p (j t) -> p j t", t=2)[:, j0:j1], m4[:, :, 0:2], m4[:, :, 2:4], ALU.add
+            )
+
+        def add_sums(u, j0, j1):
+            nc.vector.tensor_tensor(
+                sums[u][:, j0:j1], pairs[u][:, 2 * j0 : 2 * j1 : 2], pairs[u][:, 2 * j0 + 1 : 2 * j1 : 2], ALU.add
+            )
+            nc.scalar.activation(gate[u][:, j0:j1], sums[u][:, j0:j1], ACT.Tanh)
+
+        def finish(u, j0, j1):
+            nc.vector.scalar_tensor_tensor(
+                result[u][:, j0:j1], gate[u][:, j0:j1], 1.0, h_win[u][:, j0:j1], ALU.add, ALU.mult
+            )
+            nc.sync.dma_start(out=out[u * P : (u + 1) * P, j0:j1], in_=result[u][:, j0:j1])
+
+        pieces = [(0, 0, S), (1, 0, S), (2, 0, S), (3, 0, S // 2), (3, S // 2, S)]
+        halve_h(0)
+        halve_h(1)
+        for step in range(len(pieces) + 2):
+            if step < len(pieces):
+                u, j0, j1 = pieces[step]
+                fetch_h(u, range(j0 * MEMBERS // S, j1 * MEMBERS // S))
+            if step + 2 < PACK:
+                halve_h(step + 2)
+            if 2 <= step:
+                finish(*pieces[step - 2])
+            if 1 <= step <= len(pieces):
+                add_sums(*pieces[step - 1])
+            if step < len(pieces):
+                add_pairs(*pieces[step])

@@ -1,6 +1,7 @@
 from contextlib import ExitStack
 
 import concourse.mybir as mybir
+from concourse.masks import make_identity
 
 K, T, S, N, H, W = 512, 2048, 256, 512, 512, 1024
 FLOPS = 2 * K * H * S * 2 + 2 * H * N * S
@@ -19,8 +20,8 @@ P = 128
 PACK = 4
 SPARE = 16
 MEMBERS = 4
-W1_VECTOR = 80
-ON_VECTOR = ((0, 2), (0, 3), (1, 3), (2, 3), (3, 3))
+ON_VECTOR = ((0, 1), (0, 3), (1, 1), (1, 3), (2, 1), (2, 3), (3, 3))
+H_ON_VECTOR = (1, 3)
 
 
 def tile_picked_twlflowbgsumg_none_p_kernel(
@@ -36,14 +37,20 @@ def tile_picked_twlflowbgsumg_none_p_kernel(
             nc.sync.dma_start(lst[:], src)
             return lst
 
-        def load_weight(src, name):
-            raw = keep.tile([P, PACK, src.shape[1]], F32, name=name, tag=name)
-            nc.sync.dma_start(out=raw[:], in_=src.rearrange("(p j) c -> p j c", j=PACK))
-            return raw
+        def load_weight(src, name, parts):
+            width = src.shape[1] // parts
+            raws = []
+            for i in range(parts):
+                raw = keep.tile([P, PACK, width], F32, name=f"{name}{i}", tag=f"{name}{i}")
+                nc.sync.dma_start(
+                    out=raw[:], in_=src.rearrange("(p j) c -> p j c", j=PACK)[:, :, i * width : (i + 1) * width]
+                )
+                raws.append(raw)
+            return raws
 
-        def mx_tiles(width, name, tag=""):
+        def mx_tiles(width, name, tag="", codes_tag=""):
             rounded = keep.tile([P, PACK * width], BF16, name=name + "_bf16", tag=tag or name + "_bf16", align_bytes=64)
-            codes = keep.tile([P, width], U32, name=name + "_codes", tag=name + "_codes", align_bytes=64)
+            codes = keep.tile([P, width], U32, name=name + "_codes", tag=codes_tag or name + "_codes", align_bytes=64)
             scales = keep.tile([P, width], U8, name=name + "_scales", align_bytes=64)
             return rounded, codes, scales
 
@@ -55,10 +62,10 @@ def tile_picked_twlflowbgsumg_none_p_kernel(
                 in_=rounded[:, PACK * first : PACK * (first + count)],
             )
 
-        def deal(copy, raw, rounded, m0, m1):
+        def deal(copy, raw, rounded, m0, m1, base=0, tiles=slice(0, PACK)):
             copy(
-                out=rounded[:].rearrange("p (t m j) -> p m j t", t=PACK, j=PACK)[:, m0:m1],
-                in_=raw[:].rearrange("p j (m t) -> p m j t", t=PACK)[:, m0:m1],
+                out=rounded[:].rearrange("p (t m j) -> p m j t", t=PACK, j=PACK)[:, m0:m1, :, tiles],
+                in_=raw[:].rearrange("p j (m t) -> p m j t", t=PACK)[:, m0 - base : m1 - base, :, tiles],
             )
 
         def product(bank, w_tiles, t, codes, scales):
@@ -78,28 +85,31 @@ def tile_picked_twlflowbgsumg_none_p_kernel(
             return win
 
         xs = keep.tile([P, T], U8, name="xs")
-        nc.vector.memset(xs[:].bitcast(I32), 0)
+        nc.gpsimd.memset(xs[:].bitcast(I32), 0)
+        xs_in = keep.tile([P, T], U8, name="xs_in")
         for q in range(4):
-            nc.scalar.dma_start(
-                out=xs[32 * q : 32 * q + 4, :].bitcast(I32), in_=x_scales[0, 4 * q : 4 * q + 4, :].bitcast(I32)
+            nc.sync.dma_start(
+                out=xs_in[32 * q : 32 * q + 4, :].bitcast(I32), in_=x_scales[0, 4 * q : 4 * q + 4, :].bitcast(I32)
             )
         offs_l = load_list(offs, "offs_l")
-        w1_raw = load_weight(w1, "w1_raw")
         two_l = load_list(two, "two_l")
+        w1_raw = load_weight(w1, "w1_raw", 1)
         xw = keep.tile([P, T], I32, name="xw")
         nc.sync.dma_start(out=xw[:], in_=x_words[0].rearrange("p n t -> p (n t)").bitcast(I32))
         n1_l = load_list(n1, "n1_l")
         n2_l = load_list(n2, "n2_l")
-        w2_raw = load_weight(w2, "w2_raw")
+        w2_raw = load_weight(w2, "w2_raw", 2)
         n3_l = load_list(n3, "n3_l")
         gain = keep.tile([P, PACK], F32, name="gain")
         nc.sync.dma_start(out=gain[:], in_=gn.rearrange("(p t) o -> p (t o)", t=PACK))
-        w3_raw = load_weight(w3, "w3_raw")
+        w3_raw = load_weight(w3, "w3_raw", 1)
         n4_l = load_list(n4, "n4_l")
 
         y_win = [window(f"y_win{t}") for t in range(PACK)]
         d_win = [window(f"d_win{t}") for t in range(PACK)]
         h_win = [window(f"h_win{t}") for t in range(PACK)]
+        ident = keep.tile([P, P], F32, name="ident")
+        make_identity(nc, ident[:])
         half_gain = keep.tile([P, PACK], F32, name="half_gain")
         nc.gpsimd.tensor_scalar(half_gain[:], gain[:], 0.5, 0.0, ALU.mult, ALU.add)
 
@@ -111,21 +121,26 @@ def tile_picked_twlflowbgsumg_none_p_kernel(
         w2_mx = mx_tiles(H, "w2")
         z_mx = mx_tiles(S, "z")
 
+        for q in range(4):
+            rows = slice(32 * q, 32 * q + 4)
+            nc.vector.tensor_copy(xs[rows, :].bitcast(I32), xs_in[rows, :].bitcast(I32))
         nc.vector.tensor_copy(xy_scales[:], xs[:].indirect(offs_l[:]))
-        deal(nc.vector.tensor_copy, w1_raw, w1_mx[0], 0, W1_VECTOR)
-        deal(nc.scalar.copy, w1_raw, w1_mx[0], W1_VECTOR, P)
-        quantize(w1_mx, 0, H)
         nc.vector.tensor_copy(xd_scales[:], xs[:].indirect(two_l[:]))
+        for half in range(2):
+            deal(nc.vector.tensor_copy, w1_raw[0], w1_mx[0], 0, P, tiles=slice(2 * half, 2 * half + 2))
+        for half in range(2):
+            quantize(w1_mx, half * H // 2, H // 2)
         nc.vector.tensor_copy(xy_codes[:], xw[:].bitcast(U32).indirect(offs_l[:]))
         nc.vector.tensor_copy(xd_codes[:], xw[:].bitcast(U32).indirect(two_l[:]))
         y_bank = [psum.tile([P, S], F32, name=f"y_bank{t}", tag=f"bank{t}") for t in range(PACK)]
         for t in range(PACK):
             product(y_bank[t], w1_mx, t, xy_codes, xy_scales)
         nc.scalar.copy(y_win[0][:, :S], y_bank[0][:])
-        for t in (1, 2):
-            nc.vector.tensor_copy(y_win[t][:, :S], y_bank[t][:])
+        nc.vector.tensor_copy(y_win[1][:, :S], y_bank[1][:])
+        deal(nc.vector.tensor_copy, w2_raw[0], w2_mx[0], 0, P // 2)
+        nc.vector.tensor_copy(y_win[2][:, :S], y_bank[2][:])
 
-        early = keep.tile([P, 2, 2, S], F32, name="early")
+        early = keep.tile([P, 2, 2, S], F32, name="early", tag="early", align_bytes=64)
         pair = [early[:, 0], early[:, 1]]
         near = keep.tile([P, PACK, S], F32, name="near")
         far = keep.tile([P, PACK, S], F32, name="far")
@@ -135,53 +150,77 @@ def tile_picked_twlflowbgsumg_none_p_kernel(
             nc.scalar.activation(pair[t][:, 1], y_win[t][:].indirect(n2_l[:]), ACT.Copy)
 
         fetch_y(0)
-        deal(nc.vector.tensor_copy, w2_raw, w2_mx[0], 0, P)
+        for half in range(2):
+            deal(nc.vector.tensor_copy, w2_raw[1], w2_mx[0], P // 2, P, P // 2, slice(2 * half, 2 * half + 2))
         fetch_y(1)
         nc.scalar.copy(y_win[3][:, :S], y_bank[3][:])
         d_bank = [psum.tile([P, S], F32, name=f"d_bank{t}", tag=f"bank{PACK + t}") for t in range(PACK)]
+        for half in range(2):
+            quantize(w2_mx, half * H // 2, H // 2)
         for t in range(PACK):
-            quantize(w2_mx, t * P, P)
             product(d_bank[t], w2_mx, t, xd_codes, xd_scales)
 
-        late = keep.tile([P, 2, 2, S], F32, name="late", tag="w2_bf16", align_bytes=64)
-        pair.extend([late[:, 0], late[:, 1]])
-        diffs = keep.tile([P, 2 * PACK, S], F32, name="diffs", tag="w2_raw")
+        late = keep.tile([P, 5, S], F32, name="late", tag="w2_codes", align_bytes=64)
+        pair.extend([late[:, 0:2], late[:, 2:4]])
+        diffs = keep.tile([P, 2 * PACK, S], F32, name="diffs", tag="w2_raw1")
         diff = [diffs[:, i] for i in range(2 * PACK)]
-        w3_mx = mx_tiles(N, "w3", tag="w2_codes")
+        w3_mx = mx_tiles(N, "w3", tag="early", codes_tag="w2_codes")
         w3_dst = w3_mx[0][:].rearrange("p (c i j) -> p c j i", i=4, j=PACK)
-        w3_src = w3_raw[:].rearrange("p j (c i) -> p c j i", i=4)
+        w3_src = w3_raw[0][:].rearrange("p j (c i) -> p c j i", i=4)
         for t in range(PACK):
             nc.scalar.activation(d_win[t][:, :S], d_bank[t][:], ACT.Copy, scale=half_gain[:, t : t + 1])
-        fetch_y(2)
-        fetch_y(3)
-        for t in range(PACK):
-            for u in range(2):
-                nc.vector.tensor_tensor(diff[2 * t + u], pair[t][:, u], y_win[t][:, :S], ALU.subtract)
+            if t % 2 == 1:
+                fetch_y(2 + t // 2)
+        nc.scalar.activation(late[:, 4], d_win[3][:].indirect(n3_l[:]), ACT.Copy)
+        def subtract(t):
+            own = y_win[t][:, :S].unsqueeze(1).to_broadcast([P, 2, S])
+            nc.vector.tensor_tensor(diffs[:, 2 * t : 2 * t + 2], pair[t], own, ALU.subtract)
+
+        def times_near(t):
             nc.vector.scalar_tensor_tensor(near[:, t, :], diff[2 * t], 2.0, d_win[t][:, :S], ALU.mult, ALU.mult)
-            nc.vector.tensor_tensor(far[:, t, :], d_win[t][:].indirect(n3_l[:]), diff[2 * t + 1], ALU.mult)
-        for half in range(2):
-            nc.scalar.copy(out=w3_dst[:, half * 64 : (half + 1) * 64], in_=w3_src[:, half * 64 : (half + 1) * 64])
+
+        def times_far(t):
+            fetched = late[:, 4] if t == 3 else d_win[t][:].indirect(n3_l[:])
+            nc.vector.tensor_tensor(far[:, t, :], fetched, diff[2 * t + 1], ALU.mult)
+
+        subtract(0)
+        subtract(1)
+        times_near(0)
+        times_far(0)
+        times_far(1)
+        subtract(2)
+        times_near(1)
+        times_far(2)
+        subtract(3)
+        times_near(2)
+        times_near(3)
+        times_far(3)
+        for c0, c1 in ((0, 32), (32, 64), (64, 128)):
+            nc.scalar.copy(out=w3_dst[:, c0:c1], in_=w3_src[:, c0:c1])
         z_dst = z_mx[0][:].rearrange("p (c i t) -> p c t i", i=4, t=PACK)
         near_src = near[:].rearrange("p t (c i) -> p c t i", i=4)
         far_src = far[:].rearrange("p t (c i) -> p c t i", i=4)
+        quantize(w3_mx, 0, P)
         for half in range(2):
             cs = slice(half * 32, (half + 1) * 32)
             nc.vector.tensor_tensor(z_dst[:, cs], near_src[:, cs], far_src[:, cs], ALU.add)
-            quantize(w3_mx, half * 256, 256)
         for half in range(2):
             quantize(z_mx, half * P, P)
+        quantize(w3_mx, P, P)
+        quantize(w3_mx, N // 2, N // 2)
 
         h_bank = [psum.tile([P, S], F32, name=f"h_bank{u}", tag=f"bank{u}") for u in range(PACK)]
         for u in range(PACK):
             product(h_bank[u], w3_mx, u, z_mx[1], z_mx[2])
-        members = [keep.tile([P, W], F32, name=f"members{u}") for u in range(PACK)]
+        members = [keep.tile([P, W], F32, name=f"members{u}", tag=f"members{u}") for u in range(PACK)]
+        held = {}
         pairs = [keep.tile([P, W // 2], F32, name=f"pairs{u}") for u in range(PACK)]
         sums = [keep.tile([P, S], F32, name=f"sums{u}") for u in range(PACK)]
         gate = [keep.tile([P, S], F32, name=f"gate{u}") for u in range(PACK)]
         result = [keep.tile([P, S], F32, name=f"result{u}") for u in range(PACK)]
 
         def halve_h(u):
-            if u == 1:
+            if u in H_ON_VECTOR:
                 nc.vector.tensor_scalar(h_win[u][:, :S], h_bank[u][:], 0.5, 0.0, ALU.mult, ALU.add)
             else:
                 nc.scalar.activation(h_win[u][:, :S], h_bank[u][:], ACT.Copy, scale=0.5)
@@ -189,14 +228,14 @@ def tile_picked_twlflowbgsumg_none_p_kernel(
         def fetch_h(u, quarters):
             for q in quarters:
                 looked_up = h_win[u][:].indirect(n4_l[:, q * 16 : (q + 1) * 16])
-                dst = members[u][:, q * S : (q + 1) * S]
+                dst = held.get((u, q // 2), members[u])[:, q * S : (q + 1) * S]
                 if (u, q) in ON_VECTOR:
                     nc.vector.tensor_copy(dst, looked_up)
                 else:
                     nc.scalar.activation(dst, looked_up, ACT.Copy)
 
         def add_pairs(u, j0, j1):
-            m4 = members[u][:].rearrange("p (j t) -> p j t", t=MEMBERS)[:, j0:j1]
+            m4 = held.get((u, j0 // P), members[u])[:].rearrange("p (j t) -> p j t", t=MEMBERS)[:, j0:j1]
             nc.vector.tensor_tensor(
                 pairs[u][:].rearrange("p (j t) -> p j t", t=2)[:, j0:j1], m4[:, :, 0:2], m4[:, :, 2:4], ALU.add
             )
@@ -207,24 +246,59 @@ def tile_picked_twlflowbgsumg_none_p_kernel(
             )
             nc.scalar.activation(gate[u][:, j0:j1], sums[u][:, j0:j1], ACT.Tanh)
 
-        def finish(u, j0, j1):
-            nc.vector.scalar_tensor_tensor(
-                result[u][:, j0:j1], gate[u][:, j0:j1], 1.0, h_win[u][:, j0:j1], ALU.add, ALU.mult
-            )
+        def store(u, j0, j1, tanh):
+            nc.vector.scalar_tensor_tensor(result[u][:, j0:j1], tanh, 1.0, h_win[u][:, j0:j1], ALU.add, ALU.mult)
             nc.sync.dma_start(out=out[u * P : (u + 1) * P, j0:j1], in_=result[u][:, j0:j1])
 
-        pieces = [(0, 0, S), (1, 0, S), (2, 0, S), (3, 0, S // 2), (3, S // 2, S)]
+        def finish(u, j0, j1):
+            store(u, j0, j1, gate[u][:, j0:j1])
+
+        turned = {}
+
+        def add_turned(u):
+            bank = psum.tile([P, S], F32, name=f"sum_bank{u}", tag=f"bank{PACK + 2 * u}")
+            for half in range(2):
+                for t in range(MEMBERS):
+                    nc.tensor.matmul(
+                        bank[:, half * P : (half + 1) * P],
+                        lhsT=members[u][:, half * 512 + t : (half + 1) * 512 : MEMBERS],
+                        rhs=ident[:],
+                        is_transpose=True,
+                        start=(t == 0),
+                        stop=(t == MEMBERS - 1),
+                    )
+            turned[u] = bank
+
+        def gate_turned(u):
+            nc.scalar.activation(gate[u][:], turned[u][:], ACT.Tanh)
+            bank = psum.tile([P, S], F32, name=f"back_bank{u}", tag=f"bank{PACK + 2 * u + 1}")
+            for half in range(2):
+                nc.tensor.transpose(bank[:, half * P : (half + 1) * P], gate[u][:, half * P : (half + 1) * P], ident[:])
+            turned[u] = bank
+
         halve_h(0)
         halve_h(1)
-        for step in range(len(pieces) + 2):
-            if step < len(pieces):
-                u, j0, j1 = pieces[step]
-                fetch_h(u, range(j0 * MEMBERS // S, j1 * MEMBERS // S))
-            if step + 2 < PACK:
-                halve_h(step + 2)
-            if 2 <= step:
-                finish(*pieces[step - 2])
-            if 1 <= step <= len(pieces):
-                add_sums(*pieces[step - 1])
-            if step < len(pieces):
-                add_pairs(*pieces[step])
+        fetch_h(0, range(2))
+        halve_h(2)
+        fetch_h(0, range(2, 4))
+        add_turned(0)
+        fetch_h(1, range(4))
+        add_turned(1)
+        fetch_h(2, range(4))
+        halve_h(3)
+        gate_turned(0)
+        add_pairs(2, 0, S)
+        held[(3, 1)] = keep.tile([P, W], F32, name="members_last", tag="members2")
+        fetch_h(3, range(2))
+        gate_turned(1)
+        fetch_h(3, range(2, 4))
+        add_sums(2, 0, S)
+        store(0, 0, S, turned[0][:])
+        add_pairs(3, 0, S // 2)
+        store(1, 0, S, turned[1][:])
+        add_sums(3, 0, S // 2)
+        add_pairs(3, S // 2, S)
+        finish(2, 0, S)
+        add_sums(3, S // 2, S)
+        finish(3, 0, S // 2)
+        finish(3, S // 2, S)

@@ -20,7 +20,7 @@ P = 128
 PACK = 4
 SPARE = 16
 MEMBERS = 4
-ON_VECTOR = ((0, 1), (0, 3), (1, 1), (1, 3), (2, 1), (2, 3), (3, 3))
+ON_VECTOR = ()
 H_ON_VECTOR = (1, 3)
 
 
@@ -37,16 +37,10 @@ def tile_picked_twlflowbgsumg_none_p_kernel(
             nc.sync.dma_start(lst[:], src)
             return lst
 
-        def load_weight(src, name, parts):
-            width = src.shape[1] // parts
-            raws = []
-            for i in range(parts):
-                raw = keep.tile([P, PACK, width], F32, name=f"{name}{i}", tag=f"{name}{i}")
-                nc.sync.dma_start(
-                    out=raw[:], in_=src.rearrange("(p j) c -> p j c", j=PACK)[:, :, i * width : (i + 1) * width]
-                )
-                raws.append(raw)
-            return raws
+        def load_weight(src, name, c0, c1):
+            raw = keep.tile([P, PACK, c1 - c0], F32, name=name, tag=name)
+            nc.sync.dma_start(out=raw[:], in_=src.rearrange("(p j) c -> p j c", j=PACK)[:, :, c0:c1])
+            return [raw]
 
         def mx_tiles(width, name, tag="", codes_tag=""):
             rounded = keep.tile([P, PACK * width], BF16, name=name + "_bf16", tag=tag or name + "_bf16", align_bytes=64)
@@ -79,8 +73,8 @@ def tile_picked_twlflowbgsumg_none_p_kernel(
                 stop=True,
             )
 
-        def window(name):
-            win = keep.tile([P, S + SPARE], F32, name=name)
+        def window(name, offsets=S):
+            win = keep.tile([P, offsets + SPARE], F32, name=name)
             nc.gpsimd.memset(win[:, S:], 0.0)
             return win
 
@@ -93,21 +87,22 @@ def tile_picked_twlflowbgsumg_none_p_kernel(
             )
         offs_l = load_list(offs, "offs_l")
         two_l = load_list(two, "two_l")
-        w1_raw = load_weight(w1, "w1_raw", 1)
+        w1_raw = load_weight(w1, "w1_raw", 0, H)
         xw = keep.tile([P, T], I32, name="xw")
         nc.sync.dma_start(out=xw[:], in_=x_words[0].rearrange("p n t -> p (n t)").bitcast(I32))
         n1_l = load_list(n1, "n1_l")
+        w2_raw = load_weight(w2, "w2_raw", 0, H // 2)
         n2_l = load_list(n2, "n2_l")
-        w2_raw = load_weight(w2, "w2_raw", 2)
+        w2_raw += load_weight(w2, "w2_raw1", H // 2, H)
         n3_l = load_list(n3, "n3_l")
         gain = keep.tile([P, PACK], F32, name="gain")
         nc.sync.dma_start(out=gain[:], in_=gn.rearrange("(p t) o -> p (t o)", t=PACK))
-        w3_raw = load_weight(w3, "w3_raw", 1)
+        w3_raw = load_weight(w3, "w3_raw", 0, N)
         n4_l = load_list(n4, "n4_l")
 
         y_win = [window(f"y_win{t}") for t in range(PACK)]
         d_win = [window(f"d_win{t}") for t in range(PACK)]
-        h_win = [window(f"h_win{t}") for t in range(PACK)]
+        h_win = [window(f"h_win{t}", 2 * S) for t in range(PACK)]
         ident = keep.tile([P, P], F32, name="ident")
         make_identity(nc, ident[:])
         half_gain = keep.tile([P, PACK], F32, name="half_gain")
@@ -225,14 +220,13 @@ def tile_picked_twlflowbgsumg_none_p_kernel(
             else:
                 nc.scalar.activation(h_win[u][:, :S], h_bank[u][:], ACT.Copy, scale=0.5)
 
-        def fetch_h(u, quarters):
-            for q in quarters:
-                looked_up = h_win[u][:].indirect(n4_l[:, q * 16 : (q + 1) * 16])
-                dst = held.get((u, q // 2), members[u])[:, q * S : (q + 1) * S]
-                if (u, q) in ON_VECTOR:
-                    nc.vector.tensor_copy(dst, looked_up)
-                else:
-                    nc.scalar.activation(dst, looked_up, ACT.Copy)
+        def fetch_h(u, q0, q1, on_vector):
+            looked_up = h_win[u][:].indirect(n4_l[:, q0 * 16 : q1 * 16])
+            dst = held.get((u, q0 // 2), members[u])[:, q0 * S : q1 * S]
+            if on_vector:
+                nc.vector.tensor_copy(dst, looked_up)
+            else:
+                nc.scalar.activation(dst, looked_up, ACT.Copy)
 
         def add_pairs(u, j0, j1):
             m4 = held.get((u, j0 // P), members[u])[:].rearrange("p (j t) -> p j t", t=MEMBERS)[:, j0:j1]
@@ -248,7 +242,8 @@ def tile_picked_twlflowbgsumg_none_p_kernel(
 
         def store(u, j0, j1, tanh):
             nc.vector.scalar_tensor_tensor(result[u][:, j0:j1], tanh, 1.0, h_win[u][:, j0:j1], ALU.add, ALU.mult)
-            nc.sync.dma_start(out=out[u * P : (u + 1) * P, j0:j1], in_=result[u][:, j0:j1])
+            queue = nc.scalar if (u, j1) == (PACK - 1, S) else nc.sync
+            queue.dma_start(out=out[u * P : (u + 1) * P, j0:j1], in_=result[u][:, j0:j1])
 
         def finish(u, j0, j1):
             store(u, j0, j1, gate[u][:, j0:j1])
@@ -278,27 +273,34 @@ def tile_picked_twlflowbgsumg_none_p_kernel(
 
         halve_h(0)
         halve_h(1)
-        fetch_h(0, range(2))
+        fetch_h(0, 0, 1, False)
+        fetch_h(0, 1, 2, True)
         halve_h(2)
-        fetch_h(0, range(2, 4))
+        fetch_h(0, 2, 3, False)
+        fetch_h(0, 3, 4, True)
         add_turned(0)
-        fetch_h(1, range(4))
+        fetch_h(1, 0, 1, False)
+        fetch_h(1, 1, 2, True)
+        fetch_h(1, 2, 3, False)
+        fetch_h(1, 3, 4, True)
         add_turned(1)
-        fetch_h(2, range(4))
+        fetch_h(2, 0, 2, False)
+        fetch_h(2, 2, 4, True)
         halve_h(3)
         gate_turned(0)
         add_pairs(2, 0, S)
         held[(3, 1)] = keep.tile([P, W], F32, name="members_last", tag="members2")
-        fetch_h(3, range(2))
-        gate_turned(1)
-        fetch_h(3, range(2, 4))
+        fetch_h(3, 0, 2, False)
+        fetch_h(3, 2, 3, False)
+        fetch_h(3, 3, 4, True)
         add_sums(2, 0, S)
-        store(0, 0, S, turned[0][:])
         add_pairs(3, 0, S // 2)
-        store(1, 0, S, turned[1][:])
-        add_sums(3, 0, S // 2)
+        gate_turned(1)
+        store(0, 0, S, turned[0][:])
         add_pairs(3, S // 2, S)
+        add_sums(3, 0, S // 2)
         finish(2, 0, S)
         add_sums(3, S // 2, S)
+        store(1, 0, S, turned[1][:])
         finish(3, 0, S // 2)
         finish(3, S // 2, S)

@@ -73,8 +73,8 @@ def tile_picked_twlflowbgsumg_none_p_kernel(
                 stop=True,
             )
 
-        def window(name, offsets=S):
-            win = keep.tile([P, offsets + SPARE], F32, name=name)
+        def window(name, offsets=S, tag=""):
+            win = keep.tile([P, offsets + SPARE], F32, name=name, tag=tag or name)
             nc.gpsimd.memset(win[:, S:], 0.0)
             return win
 
@@ -90,23 +90,22 @@ def tile_picked_twlflowbgsumg_none_p_kernel(
         w1_raw = load_weight(w1, "w1_raw", 0, H)
         xw = keep.tile([P, T], I32, name="xw")
         nc.sync.dma_start(out=xw[:], in_=x_words[0].rearrange("p n t -> p (n t)").bitcast(I32))
+        gain = keep.tile([P, PACK], F32, name="gain")
+        nc.sync.dma_start(out=gain[:], in_=gn.rearrange("(p t) o -> p (t o)", t=PACK))
         n1_l = load_list(n1, "n1_l")
         w2_raw = load_weight(w2, "w2_raw", 0, H // 2)
         n2_l = load_list(n2, "n2_l")
         w2_raw += load_weight(w2, "w2_raw1", H // 2, H)
         n3_l = load_list(n3, "n3_l")
-        gain = keep.tile([P, PACK], F32, name="gain")
-        nc.sync.dma_start(out=gain[:], in_=gn.rearrange("(p t) o -> p (t o)", t=PACK))
         w3_raw = load_weight(w3, "w3_raw", 0, N)
         n4_l = load_list(n4, "n4_l")
 
-        y_win = [window(f"y_win{t}") for t in range(PACK)]
-        d_win = [window(f"d_win{t}") for t in range(PACK)]
-        h_win = [window(f"h_win{t}", 2 * S) for t in range(PACK)]
         ident = keep.tile([P, P], F32, name="ident")
         make_identity(nc, ident[:])
-        half_gain = keep.tile([P, PACK], F32, name="half_gain")
-        nc.gpsimd.tensor_scalar(half_gain[:], gain[:], 0.5, 0.0, ALU.mult, ALU.add)
+        y_win = [window(f"y_win{t}") for t in range(PACK)]
+        d_win = [keep.tile([P, S + SPARE], F32, name=f"d_win{t}") for t in range(PACK)]
+        for t in range(PACK):
+            nc.scalar.copy(d_win[t][:, S:], y_win[t][:, S:])
 
         xy_codes = keep.tile([P, S], U32, name="xy_codes", align_bytes=64)
         xy_scales = keep.tile([P, S], U8, name="xy_scales", align_bytes=64)
@@ -130,10 +129,10 @@ def tile_picked_twlflowbgsumg_none_p_kernel(
         y_bank = [psum.tile([P, S], F32, name=f"y_bank{t}", tag=f"bank{t}") for t in range(PACK)]
         for t in range(PACK):
             product(y_bank[t], w1_mx, t, xy_codes, xy_scales)
-        nc.scalar.copy(y_win[0][:, :S], y_bank[0][:])
-        nc.vector.tensor_copy(y_win[1][:, :S], y_bank[1][:])
+        nc.scalar.activation(y_win[0][:, :S], y_bank[0][:], ACT.Copy, scale=gain[:, 0:1])
+        nc.vector.tensor_scalar_mul(y_win[1][:, :S], y_bank[1][:], gain[:, 1:2])
         deal(nc.vector.tensor_copy, w2_raw[0], w2_mx[0], 0, P // 2)
-        nc.vector.tensor_copy(y_win[2][:, :S], y_bank[2][:])
+        nc.vector.tensor_scalar_mul(y_win[2][:, :S], y_bank[2][:], gain[:, 2:3])
 
         early = keep.tile([P, 2, 2, S], F32, name="early", tag="early", align_bytes=64)
         pair = [early[:, 0], early[:, 1]]
@@ -148,7 +147,7 @@ def tile_picked_twlflowbgsumg_none_p_kernel(
         for half in range(2):
             deal(nc.vector.tensor_copy, w2_raw[1], w2_mx[0], P // 2, P, P // 2, slice(2 * half, 2 * half + 2))
         fetch_y(1)
-        nc.scalar.copy(y_win[3][:, :S], y_bank[3][:])
+        nc.scalar.activation(y_win[3][:, :S], y_bank[3][:], ACT.Copy, scale=gain[:, 3:4])
         d_bank = [psum.tile([P, S], F32, name=f"d_bank{t}", tag=f"bank{PACK + t}") for t in range(PACK)]
         for half in range(2):
             quantize(w2_mx, half * H // 2, H // 2)
@@ -163,7 +162,7 @@ def tile_picked_twlflowbgsumg_none_p_kernel(
         w3_dst = w3_mx[0][:].rearrange("p (c i j) -> p c j i", i=4, j=PACK)
         w3_src = w3_raw[0][:].rearrange("p j (c i) -> p c j i", i=4)
         for t in range(PACK):
-            nc.scalar.activation(d_win[t][:, :S], d_bank[t][:], ACT.Copy, scale=half_gain[:, t : t + 1])
+            nc.scalar.activation(d_win[t][:, :S], d_bank[t][:], ACT.Copy, scale=0.5)
             if t % 2 == 1:
                 fetch_y(2 + t // 2)
         nc.scalar.activation(late[:, 4], d_win[3][:].indirect(n3_l[:]), ACT.Copy)
@@ -204,6 +203,7 @@ def tile_picked_twlflowbgsumg_none_p_kernel(
         quantize(w3_mx, P, P)
         quantize(w3_mx, N // 2, N // 2)
 
+        h_win = [window(f"h_win{t}", 2 * S, f"y_win{t}") for t in range(PACK)]
         h_bank = [psum.tile([P, S], F32, name=f"h_bank{u}", tag=f"bank{u}") for u in range(PACK)]
         for u in range(PACK):
             product(h_bank[u], w3_mx, u, z_mx[1], z_mx[2])

from contextlib import ExitStack

import concourse.mybir as mybir
from concourse.masks import make_identity

K, T, S, N, H, W = 512, 2048, 256, 512, 512, 1024
FLOPS = 2 * K * H * S * 2 + 2 * H * N * S

F32 = mybir.dt.float32
BF16 = mybir.dt.bfloat16
I32 = mybir.dt.int32
U32 = mybir.dt.uint32
U16 = mybir.dt.uint16
U8 = mybir.dt.uint8
FP8X4 = mybir.dt.float8_e4m3fn_x4
ALU = mybir.AluOpType
ACT = mybir.ActivationFunctionType

P = 128
PACK = 4
SPARE = 16
MEMBERS = 4
ON_VECTOR = ()
H_ON_VECTOR = (1, 3)


def tile_picked_twlflowbgsumg_none_p_kernel(
    tc, x_words, x_scales, w1, w2, gn, w3, offs, two, n1, n2, n3, n4, out
):
    nc = tc.nc
    with ExitStack() as ctx:
        keep = ctx.enter_context(tc.tile_pool(name="keep", bufs=1))
        psum = ctx.enter_context(tc.psum_pool(name="psum", bufs=1))

        def load_list(src, name):
            lst = keep.tile([P, src.shape[1]], U16, name=name)
            nc.sync.dma_start(lst[:], src)
            return lst

        def load_weight(src, name, c0, c1):
            raw = keep.tile([P, PACK, c1 - c0], F32, name=name, tag=name)
            nc.sync.dma_start(out=raw[:], in_=src.rearrange("(p j) c -> p j c", j=PACK)[:, :, c0:c1])
            return [raw]

        def mx_tiles(width, name, tag="", codes_tag=""):
            rounded = keep.tile([P, PACK * width], BF16, name=name + "_bf16", tag=tag or name + "_bf16", align_bytes=64)
            codes = keep.tile([P, width], U32, name=name + "_codes", tag=codes_tag or name + "_codes", align_bytes=64)
            scales = keep.tile([P, width], U8, name=name + "_scales", align_bytes=64)
            return rounded, codes, scales

        def quantize(tiles, first, count):
            rounded, codes, scales = tiles
            nc.vector.quantize_mx(
                out=codes[:, first : first + count].bitcast(FP8X4),
                scales=scales[:, first : first + count],
                in_=rounded[:, PACK * first : PACK * (first + count)],
            )

        def deal(copy, raw, rounded, m0, m1, base=0, tiles=slice(0, PACK)):
            copy(
                out=rounded[:].rearrange("p (t m j) -> p m j t", t=PACK, j=PACK)[:, m0:m1, :, tiles],
                in_=raw[:].rearrange("p j (m t) -> p m j t", t=PACK)[:, m0 - base : m1 - base, :, tiles],
            )

        def product(bank, w_tiles, t, codes, scales):
            nc.tensor.matmul_mx(
                out=bank[:],
                lhsT=w_tiles[1][:, t * P : (t + 1) * P].bitcast(FP8X4),
                lhsT_scale=w_tiles[2][:, t * P : (t + 1) * P],
                rhs=codes[:].bitcast(FP8X4),
                rhs_scale=scales[:],
                start=True,
                stop=True,
            )

        def window(name, offsets=S, tag=""):
            win = keep.tile([P, offsets + SPARE], F32, name=name, tag=tag or name)
            nc.gpsimd.memset(win[:, S:], 0.0)
            return win

        xs = keep.tile([P, T], U8, name="xs")
        nc.gpsimd.memset(xs[:].bitcast(I32), 0)
        xs_in = keep.tile([P, T], U8, name="xs_in")
        for q in range(4):
            nc.sync.dma_start(
                out=xs_in[32 * q : 32 * q + 4, :].bitcast(I32), in_=x_scales[0, 4 * q : 4 * q + 4, :].bitcast(I32)
            )
        offs_l = load_list(offs, "offs_l")
        two_l = load_list(two, "two_l")
        w1_raw = load_weight(w1, "w1_raw", 0, H)
        xw = keep.tile([P, T], I32, name="xw")
        nc.sync.dma_start(out=xw[:], in_=x_words[0].rearrange("p n t -> p (n t)").bitcast(I32))
        gain = keep.tile([P, PACK], F32, name="gain")
        nc.sync.dma_start(out=gain[:], in_=gn.rearrange("(p t) o -> p (t o)", t=PACK))
        n1_l = load_list(n1, "n1_l")
        w2_raw = load_weight(w2, "w2_raw", 0, H // 2)
        n2_l = load_list(n2, "n2_l")
        w2_raw += load_weight(w2, "w2_raw1", H // 2, H)
        n3_l = load_list(n3, "n3_l")
        w3_raw = load_weight(w3, "w3_raw", 0, N)
        n4_l = load_list(n4, "n4_l")

        ident = keep.tile([P, P], F32, name="ident")
        make_identity(nc, ident[:])
        y_win = [window(f"y_win{t}") for t in range(PACK)]
        d_win = [keep.tile([P, S + SPARE], F32, name=f"d_win{t}") for t in range(PACK)]
        for t in range(PACK):
            nc.scalar.copy(d_win[t][:, S:], y_win[t][:, S:])

        xy_codes = keep.tile([P, S], U32, name="xy_codes", align_bytes=64)
        xy_scales = keep.tile([P, S], U8, name="xy_scales", align_bytes=64)
        xd_codes = keep.tile([P, S], U32, name="xd_codes", align_bytes=64)
        xd_scales = keep.tile([P, S], U8, name="xd_scales", align_bytes=64)
        w1_mx = mx_tiles(H, "w1")
        w2_mx = mx_tiles(H, "w2")
        z_mx = mx_tiles(S, "z")

        for q in range(4):
            rows = slice(32 * q, 32 * q + 4)
            nc.vector.tensor_copy(xs[rows, :].bitcast(I32), xs_in[rows, :].bitcast(I32))
        nc.vector.tensor_copy(xy_scales[:], xs[:].indirect(offs_l[:]))
        nc.vector.tensor_copy(xd_scales[:], xs[:].indirect(two_l[:]))
        for half in range(2):
            deal(nc.vector.tensor_copy, w1_raw[0], w1_mx[0], 0, P, tiles=slice(2 * half, 2 * half + 2))
        for half in range(2):
            quantize(w1_mx, half * H // 2, H // 2)
        nc.vector.tensor_copy(xy_codes[:], xw[:].bitcast(U32).indirect(offs_l[:]))
        nc.vector.tensor_copy(xd_codes[:], xw[:].bitcast(U32).indirect(two_l[:]))
        y_bank = [psum.tile([P, S], F32, name=f"y_bank{t}", tag=f"bank{t}") for t in range(PACK)]
        for t in range(PACK):
            product(y_bank[t], w1_mx, t, xy_codes, xy_scales)
        nc.scalar.activation(y_win[0][:, :S], y_bank[0][:], ACT.Copy, scale=gain[:, 0:1])
        nc.vector.tensor_scalar_mul(y_win[1][:, :S], y_bank[1][:], gain[:, 1:2])
        deal(nc.vector.tensor_copy, w2_raw[0], w2_mx[0], 0, P // 2)
        nc.vector.tensor_scalar_mul(y_win[2][:, :S], y_bank[2][:], gain[:, 2:3])

        early = keep.tile([P, 2, 2, S], F32, name="early", tag="early", align_bytes=64)
        pair = [early[:, 0], early[:, 1]]
        near = keep.tile([P, PACK, S], F32, name="near")
        far = keep.tile([P, PACK, S], F32, name="far")

        def fetch_y(t):
            nc.scalar.activation(pair[t][:, 0], y_win[t][:].indirect(n1_l[:]), ACT.Copy)
            nc.scalar.activation(pair[t][:, 1], y_win[t][:].indirect(n2_l[:]), ACT.Copy)

        fetch_y(0)
        for half in range(2):
            deal(nc.vector.tensor_copy, w2_raw[1], w2_mx[0], P // 2, P, P // 2, slice(2 * half, 2 * half + 2))
        fetch_y(1)
        nc.scalar.activation(y_win[3][:, :S], y_bank[3][:], ACT.Copy, scale=gain[:, 3:4])
        d_bank = [psum.tile([P, S], F32, name=f"d_bank{t}", tag=f"bank{PACK + t}") for t in range(PACK)]
        for half in range(2):
            quantize(w2_mx, half * H // 2, H // 2)
        for t in range(PACK):
            product(d_bank[t], w2_mx, t, xd_codes, xd_scales)

        late = keep.tile([P, 5, S], F32, name="late", tag="w2_codes", align_bytes=64)
        pair.extend([late[:, 0:2], late[:, 2:4]])
        diffs = keep.tile([P, 2 * PACK, S], F32, name="diffs", tag="w2_raw1")
        diff = [diffs[:, i] for i in range(2 * PACK)]
        w3_mx = mx_tiles(N, "w3", tag="early", codes_tag="w2_codes")
        w3_dst = w3_mx[0][:].rearrange("p (c i j) -> p c j i", i=4, j=PACK)
        w3_src = w3_raw[0][:].rearrange("p j (c i) -> p c j i", i=4)
        for t in range(PACK):
            nc.scalar.activation(d_win[t][:, :S], d_bank[t][:], ACT.Copy, scale=0.5)
            if t % 2 == 1:
                fetch_y(2 + t // 2)
        nc.scalar.activation(late[:, 4], d_win[3][:].indirect(n3_l[:]), ACT.Copy)
        def subtract(t):
            own = y_win[t][:, :S].unsqueeze(1).to_broadcast([P, 2, S])
            nc.vector.tensor_tensor(diffs[:, 2 * t : 2 * t + 2], pair[t], own, ALU.subtract)

        def times_near(t):
            nc.vector.scalar_tensor_tensor(near[:, t, :], diff[2 * t], 2.0, d_win[t][:, :S], ALU.mult, ALU.mult)

        def times_far(t):
            fetched = late[:, 4] if t == 3 else d_win[t][:].indirect(n3_l[:])
            nc.vector.tensor_tensor(far[:, t, :], fetched, diff[2 * t + 1], ALU.mult)

        subtract(0)
        subtract(1)
        times_near(0)
        times_far(0)
        times_far(1)
        subtract(2)
        times_near(1)
        times_far(2)
        subtract(3)
        times_near(2)
        times_near(3)
        times_far(3)
        for c0, c1 in ((0, 32), (32, 64), (64, 128)):
            nc.scalar.copy(out=w3_dst[:, c0:c1], in_=w3_src[:, c0:c1])
        z_dst = z_mx[0][:].rearrange("p (c i t) -> p c t i", i=4, t=PACK)
        near_src = near[:].rearrange("p t (c i) -> p c t i", i=4)
        far_src = far[:].rearrange("p t (c i) -> p c t i", i=4)
        quantize(w3_mx, 0, P)
        for half in range(2):
            cs = slice(half * 32, (half + 1) * 32)
            nc.vector.tensor_tensor(z_dst[:, cs], near_src[:, cs], far_src[:, cs], ALU.add)
        for half in range(2):
            quantize(z_mx, half * P, P)
        quantize(w3_mx, P, P)
        quantize(w3_mx, N // 2, N // 2)

        h_win = [window(f"h_win{t}", 2 * S, f"y_win{t}") for t in range(PACK)]
        h_bank = [psum.tile([P, S], F32, name=f"h_bank{u}", tag=f"bank{u}") for u in range(PACK)]
        for u in range(PACK):
            product(h_bank[u], w3_mx, u, z_mx[1], z_mx[2])
        members = [keep.tile([P, W], F32, name=f"members{u}", tag=f"members{u}") for u in range(PACK)]
        held = {}
        pairs = [keep.tile([P, W // 2], F32, name=f"pairs{u}") for u in range(PACK)]
        sums = [keep.tile([P, S], F32, name=f"sums{u}") for u in range(PACK)]
        gate = [keep.tile([P, S], F32, name=f"gate{u}") for u in range(PACK)]
        result = [keep.tile([P, S], F32, name=f"result{u}") for u in range(PACK)]

        def halve_h(u):
            if u in H_ON_VECTOR:
                nc.vector.tensor_scalar(h_win[u][:, :S], h_bank[u][:], 0.5, 0.0, ALU.mult, ALU.add)
            else:
                nc.scalar.activation(h_win[u][:, :S], h_bank[u][:], ACT.Copy, scale=0.5)

        def fetch_h(u, q0, q1, on_vector):
            looked_up = h_win[u][:].indirect(n4_l[:, q0 * 16 : q1 * 16])
            dst = held.get((u, q0 // 2), members[u])[:, q0 * S : q1 * S]
            if on_vector:
                nc.vector.tensor_copy(dst, looked_up)
            else:
                nc.scalar.activation(dst, looked_up, ACT.Copy)

        def add_pairs(u, j0, j1):
            m4 = held.get((u, j0 // P), members[u])[:].rearrange("p (j t) -> p j t", t=MEMBERS)[:, j0:j1]
            nc.vector.tensor_tensor(
                pairs[u][:].rearrange("p (j t) -> p j t", t=2)[:, j0:j1], m4[:, :, 0:2], m4[:, :, 2:4], ALU.add
            )

        def add_sums(u, j0, j1):
            nc.vector.tensor_tensor(
                sums[u][:, j0:j1], pairs[u][:, 2 * j0 : 2 * j1 : 2], pairs[u][:, 2 * j0 + 1 : 2 * j1 : 2], ALU.add
            )
            nc.scalar.activation(gate[u][:, j0:j1], sums[u][:, j0:j1], ACT.Tanh)

        def store(u, j0, j1, tanh):
            nc.vector.scalar_tensor_tensor(result[u][:, j0:j1], tanh, 1.0, h_win[u][:, j0:j1], ALU.add, ALU.mult)
            queue = nc.scalar if (u, j1) == (PACK - 1, S) else nc.sync
            queue.dma_start(out=out[u * P : (u + 1) * P, j0:j1], in_=result[u][:, j0:j1])

        def finish(u, j0, j1):
            store(u, j0, j1, gate[u][:, j0:j1])

        turned = {}

        def add_turned(u):
            bank = psum.tile([P, S], F32, name=f"sum_bank{u}", tag=f"bank{PACK + 2 * u}")
            for half in range(2):
                for t in range(MEMBERS):
                    nc.tensor.matmul(
                        bank[:, half * P : (half + 1) * P],
                        lhsT=members[u][:, half * 512 + t : (half + 1) * 512 : MEMBERS],
                        rhs=ident[:],
                        is_transpose=True,
                        start=(t == 0),
                        stop=(t == MEMBERS - 1),
                    )
            turned[u] = bank

        def gate_turned(u):
            nc.scalar.activation(gate[u][:], turned[u][:], ACT.Tanh)
            bank = psum.tile([P, S], F32, name=f"back_bank{u}", tag=f"bank{PACK + 2 * u + 1}")
            for half in range(2):
                nc.tensor.transpose(bank[:, half * P : (half + 1) * P], gate[u][:, half * P : (half + 1) * P], ident[:])
            turned[u] = bank

        halve_h(0)
        halve_h(1)
        fetch_h(0, 0, 1, False)
        fetch_h(0, 1, 2, True)
        halve_h(2)
        fetch_h(0, 2, 3, False)
        fetch_h(0, 3, 4, True)
        add_turned(0)
        fetch_h(1, 0, 1, False)
        fetch_h(1, 1, 2, True)
        fetch_h(1, 2, 3, False)
        fetch_h(1, 3, 4, True)
        add_turned(1)
        fetch_h(2, 0, 2, False)
        fetch_h(2, 2, 4, True)
        halve_h(3)
        gate_turned(0)
        add_pairs(2, 0, S)
        held[(3, 1)] = keep.tile([P, W], F32, name="members_last", tag="members2")
        fetch_h(3, 0, 2, False)
        fetch_h(3, 2, 3, False)
        fetch_h(3, 3, 4, True)
        add_sums(2, 0, S)
        add_pairs(3, 0, S // 2)
        gate_turned(1)
        store(0, 0, S, turned[0][:])
        add_pairs(3, S // 2, S)
        add_sums(3, 0, S // 2)
        finish(2, 0, S)
        add_sums(3, S // 2, S)
        store(1, 0, S, turned[1][:])
        finish(3, 0, S // 2)
        finish(3, S // 2, S)
